import numpy as np
import ml_dtypes


def mxq(x, axis, fmt="e4m3"):
    dtype, down = {"e4m3": (ml_dtypes.float8_e4m3fn, 7), "e5m2": (ml_dtypes.float8_e5m2, 14)}[fmt]
    v = np.moveaxis(np.asarray(x, np.float32).astype(ml_dtypes.bfloat16).astype(np.float64), axis, -1)
    blocks = v.reshape(v.shape[:-1] + (-1, 32))
    amax = np.abs(blocks).max(-1, keepdims=True)
    byte = np.maximum(np.where(amax > 0, np.frexp(amax)[1] - 1 + 127, 0) - down, 1)
    scale = np.exp2(byte - 127.0)
    codes = (blocks / scale).astype(np.float32).astype(dtype).astype(np.float64)
    return np.moveaxis((codes * scale).reshape(v.shape), -1, axis)


WIDE = False


def mx_kscale(k):
    if not WIDE:
        return np.ones(k)
    levels = np.array([10, -10, 5, -5, 0])
    if k % 512:
        return np.exp2(np.random.permutation(np.resize(levels, k // 32))).repeat(32)
    a = np.empty((k // 512, 16))
    for p in range(k // 512):
        a[p, :8] = np.random.permutation(np.resize(levels, 8))
        for g in range(8):
            far = levels[np.abs(levels - a[p, g]) >= 10]
            a[p, g + 8] = far[np.random.randint(len(far))]
    return np.exp2(a.ravel()).repeat(32)


def f64(x):
    return np.asarray(x).astype(np.float64)


def striped(idx):
    return np.tile(idx.reshape(-1, 16).T, (8, 1)).astype(np.uint16)


def unstriped(offs):
    return offs[:16].T.reshape(-1).astype(np.int64)


def striped8(idx):
    return np.concatenate([x.reshape(-1, 16).T for x in idx]).astype(np.uint16)


def runs(offs, k):
    lists = np.stack([offs[16 * r : 16 * r + 16].T.reshape(-1) for r in range(8)]).astype(np.int64)
    return lists[np.arange(k) % 512 // 64]


def pack_weight(w):
    k, n = w.shape
    w = f64(np.asarray(w, np.float32).astype(ml_dtypes.bfloat16)).reshape(k // 32, 32, n)
    amax = np.abs(w).max(1)
    byte = np.clip(np.where(amax > 0, np.frexp(amax)[1] - 1 + 127 - 7, 1), 1, 254)
    scaled = (w * np.exp2(127.0 - byte)[:, None, :]).reshape(k, n).astype(np.float32)
    words = np.ascontiguousarray(scaled.reshape(k // 512, 128, 4, n).transpose(0, 1, 3, 2)).astype(ml_dtypes.float8_e4m3fn).view(np.uint8)
    return words, np.ascontiguousarray(byte.astype(np.uint8).reshape(k // 512, 16, n))


def unpack_weight(words, scales):
    g, p, n, _ = words.shape
    vals = np.ascontiguousarray(words).view(ml_dtypes.float8_e4m3fn).astype(np.float64) * np.repeat(np.exp2(scales.astype(np.float64) - 127.0), 8, axis=1)[..., None]
    return vals.transpose(0, 1, 3, 2).reshape(g * 512, n)


def sigmoid(v):
    return 1.0 / (1.0 + np.exp(-np.maximum(v, -700.0)))


K, T, S, N, H, G = 512, 2048, 512, 512, 512, 2048


def setup_inputs():
    n = np.random.standard_normal
    s = mx_kscale(K)[:, None]
    u = mx_kscale(S)
    packed_xT = pack_weight(n((K, T)) * s)
    packed_dT = pack_weight(n((K, G)) / s)
    return {
        "x_words": packed_xT[0],
        "x_scales": packed_xT[1],
        "w1": (n((K, H)) / np.sqrt(K) / s).astype(np.float32),
        "d_words": packed_dT[0],
        "d_scales": packed_dT[1],
        "gn": (np.random.uniform(0.5, 1.5, (H, 1)) * u[:, None]).astype(np.float32),
        "w2": (n((H, N)) / np.sqrt(H) / u[:, None]).astype(np.float32),
        "offs": striped(np.random.permutation(T)[:S]),
        "k1": striped8(np.random.randint(0, G, (8, H))),
        "two": striped(np.random.permutation(T)[:S]),
        "n1": striped(np.random.permutation(S)),
        "n2": striped(np.random.permutation(S)),
        "n3": striped(np.random.permutation(S)),
        "n4": striped(np.random.permutation(S)),
    }


def reference(x_words, x_scales, w1, d_words, d_scales, gn, w2, offs, k1, two, n1, n2, n3, n4):
    xq = unpack_weight(x_words, x_scales)[:, unstriped(offs)]
    y = mxq(f64(w1), 0, "e4m3").T @ xq
    d_k1 = unpack_weight(d_words, d_scales)[np.arange(K)[:, None], runs(k1, K)]
    x_two = unpack_weight(x_words, x_scales)[:, unstriped(two)]
    d = 0.0625 * (d_k1.T @ x_two)
    z = f64(gn) * (y * (np.tanh(d[:, unstriped(n1)] - d[:, unstriped(n2)])))
    h = mxq(f64(w2), 0, "e4m3").T @ mxq(z, 0, "e4m3")
    return h + (sigmoid(h[:, unstriped(n3)])) * (h[:, unstriped(n4)] - h)

@@ -1,0 +1,273 @@
+from contextlib import ExitStack
+
+import concourse.mybir as mybir
+
+F32 = mybir.dt.float32
+BF16 = mybir.dt.bfloat16
+I32 = mybir.dt.int32
+U32 = mybir.dt.uint32
+U16 = mybir.dt.uint16
+U8 = mybir.dt.uint8
+FP8X4 = mybir.dt.float8_e4m3fn_x4
+ACT = mybir.ActivationFunctionType
+ALU = mybir.AluOpType
+
+P = 128
+PACK = 4
+K = 512
+TABLE = 2048
+S = 512
+HALF = S // 2
+SPARE = 16
+FLOPS = 3 * 2 * 512 * 512 * 512
+
+
+def tile_picked_twkeyjointbtrack_none_p_kernel(
+    tc, x_words, x_scales, w1, d_words, d_scales, gn, w2, offs, k1, two, n1, n2, n3, n4, out
+):
+    nc = tc.nc
+    with ExitStack() as ctx:
+        keep = ctx.enter_context(tc.tile_pool(name="keep", bufs=1))
+        ring = ctx.enter_context(tc.tile_pool(name="ring", bufs=3))
+        psum = ctx.enter_context(tc.psum_pool(name="psum", bufs=1))
+
+        def load_list(name, src):
+            tile = keep.tile([P, S // 16], U16, name=name)
+            nc.sync.dma_start(tile[:], src)
+            return tile
+
+        def load_words(name, src):
+            tile = keep.tile([P, TABLE], U32, name=name, tag=name, align_bytes=64)
+            nc.sync.dma_start(tile[:].bitcast(I32), src[0].rearrange("p c r -> p (c r)").bitcast(I32))
+            return tile
+
+        def load_weight(name, src, tag):
+            tile = keep.tile([P, PACK, S], F32, name=name, tag=tag, align_bytes=64)
+            nc.sync.dma_start(tile[:], src.rearrange("(p j) n -> p j n", j=PACK))
+            return tile
+
+        ds_table = keep.tile([P, TABLE], U8, name="ds_table", align_bytes=64)
+        xs_table = keep.tile([P, TABLE], U8, name="xs_table", align_bytes=64)
+        d_scale = keep.tile([P, S], U8, name="d_scale", align_bytes=64)
+        nc.vector.memset(ds_table[:].bitcast(I32), 0)
+        nc.vector.memset(xs_table[:].bitcast(I32), 0)
+
+        k1_l = load_list("k1_l", k1)
+        two_l = load_list("two_l", two)
+        n2_l = load_list("n2_l", n2)
+        n1_l = load_list("n1_l", n1)
+        ds_rows = d_scales[0].bitcast(I32)
+        for e in range(2):
+            nc.sync.dma_start(ds_table[:].bitcast(I32)[e:P:16, :], ds_rows[e:16:2, :])
+        dw_table = load_words("dw_table", d_words)
+        xs_rows = x_scales[0].bitcast(I32)
+        for q in range(4):
+            nc.sync.dma_start(xs_table[:].bitcast(I32)[32 * q : 32 * q + 4, :], xs_rows[4 * q : 4 * q + 4, :])
+        n3_l = load_list("n3_l", n3)
+        n4_l = load_list("n4_l", n4)
+        xw_table = load_words("xw_table", x_words)
+        offs_l = load_list("offs_l", offs)
+        gain = keep.tile([P, PACK], F32, name="gain")
+        nc.gpsimd.dma_start(gain[:], gn.rearrange("(p t) o -> p (t o)", t=PACK))
+
+        def gather(name, dtype, table, lst, tag=None):
+            tile = keep.tile([P, S], dtype, name=name, tag=tag or name, align_bytes=64)
+            nc.vector.tensor_copy(tile[:], table[:].indirect(lst[:]))
+            return tile
+
+        def quantize(name, grouped, width):
+            codes = keep.tile([P, width], U32, name=name + "_codes", align_bytes=64)
+            scales = keep.tile([P, width], U8, name=name + "_scales", align_bytes=64)
+            nc.vector.quantize_mx(out=codes[:].bitcast(FP8X4), scales=scales[:], in_=grouped[:])
+            return codes, scales
+
+        def product(dst, stat, t, moving):
+            cols = slice(t * P, (t + 1) * P)
+            nc.tensor.matmul_mx(
+                out=dst, lhsT=stat[0][:, cols].bitcast(FP8X4), lhsT_scale=stat[1][:, cols],
+                rhs=moving[0][:].bitcast(FP8X4), rhs_scale=moving[1][:], start=True, stop=True,
+            )
+
+        ds_picked = gather("ds_picked", U8, ds_table, k1_l, tag="weight")
+        nc.vector.tensor_copy(
+            d_scale[:].rearrange("p (t m) -> p t m", t=PACK), ds_picked[:].rearrange("p (m t) -> p t m", t=PACK)
+        )
+        for e in range(2):
+            nc.sync.dma_start(d_scale[:].bitcast(I32)[2 + e : P : 32, :], d_scale[:].bitcast(I32)[16 + e : P : 32, :])
+        w1_raw = load_weight("w1_raw", w1, "weight")
+
+        dw_picked = gather("dw_picked", U32, dw_table, k1_l)
+        xs_two = gather("xs_two", U8, xs_table, two_l)
+        d_codes = keep.tile([P, S], U32, name="d_codes", align_bytes=64)
+        nc.vector.tensor_copy(
+            d_codes[:].rearrange("p (t a b) -> p a t b", t=PACK, b=4),
+            dw_picked[:].rearrange("p (a b t) -> p a t b", t=PACK, b=4),
+        )
+        xw_two = gather("xw_two", U32, xw_table, two_l)
+        d_acc = []
+        for t in range(PACK):
+            acc = psum.tile([P, S], F32, name="d_acc%d" % t, tag="left%d" % t)
+            product(acc[:], (d_codes, d_scale), t, (xw_two, xs_two))
+            d_acc.append(acc)
+        xs_offs = gather("xs_offs", U8, xs_table, offs_l)
+        xw_offs = gather("xw_offs", U32, xw_table, offs_l)
+
+        y_acc = []
+        w2_q = []
+
+        def first_layer():
+            w1_grouped = keep.tile([P, PACK * S], BF16, name="w1_grouped", align_bytes=64)
+            nc.vector.tensor_copy(
+                w1_grouped[:].rearrange("p (t m j) -> p m t j", t=PACK, j=PACK),
+                w1_raw[:].rearrange("p j (m t) -> p m t j", t=PACK),
+            )
+            w1_q = quantize("w1", w1_grouped, S)
+            for t in range(PACK):
+                acc = psum.tile([P, S], F32, name="y_acc%d" % t, tag="right%d" % t)
+                product(acc[:], w1_q, t, (xw_offs, xs_offs))
+                y_acc.append(acc)
+
+        def second_weights():
+            w2_raw = load_weight("w2_raw", w2, "dw_table")
+            w2_grouped = keep.tile([P, PACK * S], BF16, name="w2_grouped", align_bytes=64)
+            nc.vector.tensor_copy(
+                w2_grouped[:].rearrange("p (c i j) -> p c j i", i=4, j=PACK),
+                w2_raw[:].rearrange("p j (c i) -> p c j i", i=4),
+            )
+            w2_q.extend(quantize("w2", w2_grouped, S))
+
+        def window(name):
+            tile = keep.tile([P, S + SPARE], F32, name=name)
+            nc.gpsimd.memset(tile[:, S:], 0.0)
+            return tile
+
+        def entries(lst, lo, hi):
+            return lst[:, lo // 16 : hi // 16]
+
+        first_layer()
+        d_rows = [window("d_row%d" % t) for t in range(PACK)]
+        h_rows = [window("h_row%d" % t) for t in range(PACK)]
+        y_gain = keep.tile([P, PACK, S], F32, name="y_gain")
+        minus = keep.tile([P, PACK, S], F32, name="minus")
+        diff = keep.tile([P, PACK, S], F32, name="diff", tag="weight", align_bytes=64)
+        gate = keep.tile([P, PACK, S], F32, name="gate")
+        h_acc = []
+
+        def difference(t, lo, hi):
+            nc.scalar.activation(minus[:, t, lo:hi], d_rows[t][:].indirect(entries(n2_l, lo, hi)), ACT.Copy, scale=-1.0)
+            nc.vector.tensor_tensor(
+                diff[:, t, lo:hi], d_rows[t][:].indirect(entries(n1_l, lo, hi)), minus[:, t, lo:hi], ALU.add
+            )
+
+        def squash(t, lo, hi):
+            nc.scalar.activation(gate[:, t, lo:hi], diff[:, t, lo:hi], ACT.Tanh, scale=0.0625)
+
+        def gained(t):
+            nc.scalar.activation(y_gain[:, t, :], y_acc[t][:], ACT.Copy, scale=gain[:, t : t + 1])
+
+        def second_layer(lo, hi):
+            z_grouped = keep.tile([P, PACK * (hi - lo)], BF16, name="z_grouped%d" % lo, align_bytes=64)
+            nc.vector.tensor_tensor(
+                z_grouped[:].rearrange("p (c i t) -> p c t i", i=2, t=PACK),
+                y_gain[:, :, lo:hi].rearrange("p t (c i) -> p c t i", i=2),
+                gate[:, :, lo:hi].rearrange("p t (c i) -> p c t i", i=2),
+                ALU.mult,
+            )
+            z_q = quantize("z%d" % lo, z_grouped, hi - lo)
+            for t in range(PACK):
+                product(h_acc[t][:, lo:hi], w2_q, t, z_q)
+
+        def fetch_h(t, lo, hi, on_vector):
+            if on_vector:
+                nc.vector.tensor_copy(h_rows[t][:, lo:hi], h_acc[t][:, lo:hi])
+            else:
+                nc.scalar.copy(h_rows[t][:, lo:hi], h_acc[t][:, lo:hi])
+
+        nc.scalar.copy(d_rows[0][:, :S], d_acc[0][:])
+        difference(0, 0, S)
+        nc.scalar.copy(d_rows[1][:, :S], d_acc[1][:])
+        difference(1, 0, S)
+        squash(0, 0, S)
+        nc.scalar.copy(d_rows[2][:, :S], d_acc[2][:])
+        difference(2, 0, HALF)
+        nc.scalar.copy(d_rows[3][:, :S], d_acc[3][:])
+        difference(3, 0, HALF)
+        squash(1, 0, S)
+        for t in range(PACK):
+            h_acc.append(psum.tile([P, S], F32, name="h_acc%d" % t, tag="left%d" % t))
+        gained(0)
+        gained(1)
+        second_weights()
+        squash(2, 0, HALF)
+        gained(2)
+        squash(3, 0, HALF)
+        gained(3)
+        difference(2, HALF, S)
+        second_layer(0, HALF)
+        difference(3, HALF, S)
+        squash(2, HALF, S)
+        squash(3, HALF, S)
+        for t in range(PACK):
+            fetch_h(t, 0, HALF, False)
+        second_layer(HALF, S)
+
+        mix = keep.tile([P, PACK, S], F32, name="mix")
+        other = keep.tile([P, PACK, S], F32, name="other")
+        first = keep.tile([P, PACK, S], F32, name="first")
+        part = keep.tile([P, PACK, S], F32, name="part")
+        result = keep.tile([P, PACK, S], F32, name="result")
+
+        def weight(t, lo, hi):
+            nc.scalar.activation(mix[:, t, lo:hi], h_rows[t][:].indirect(entries(n3_l, lo, hi)), ACT.Sigmoid)
+
+        def neighbour(t, lo, hi, on_vector):
+            looked_up = h_rows[t][:].indirect(entries(n4_l, lo, hi))
+            if on_vector:
+                nc.vector.tensor_copy(other[:, t, lo:hi], looked_up)
+            else:
+                nc.scalar.activation(other[:, t, lo:hi], looked_up, ACT.Copy)
+
+        def theirs(t, lo, hi, fused):
+            src = h_rows[t][:].indirect(entries(n4_l, lo, hi)) if fused else other[:, t, lo:hi]
+            nc.vector.tensor_tensor(first[:, t, lo:hi], src, mix[:, t, lo:hi], ALU.mult)
+
+        def ours(t, lo, hi):
+            nc.vector.scalar_tensor_tensor(
+                part[:, t, lo:hi], mix[:, t, lo:hi], 1.0, h_acc[t][:, lo:hi], ALU.subtract, ALU.mult
+            )
+
+        def finish(t, lo, hi):
+            nc.vector.tensor_tensor(result[:, t, lo:hi], first[:, t, lo:hi], part[:, t, lo:hi], ALU.subtract)
+            nc.sync.dma_start(out[t * P : (t + 1) * P, lo:hi], result[:, t, lo:hi])
+
+        fetch_h(0, HALF, S, True)
+        weight(0, 0, HALF)
+        neighbour(0, 0, HALF, True)
+        weight(0, HALF, S)
+        fetch_h(1, HALF, S, False)
+        theirs(0, 0, HALF, False)
+        weight(1, 0, HALF)
+        theirs(0, HALF, S, True)
+        weight(1, HALF, S)
+        ours(0, 0, S)
+        fetch_h(2, HALF, S, False)
+        theirs(1, 0, S, True)
+        finish(0, 0, S)
+        weight(2, 0, HALF)
+        weight(2, HALF, S)
+        ours(1, 0, S)
+        neighbour(2, 0, S, False)
+        fetch_h(3, HALF, S, False)
+        weight(3, 0, HALF)
+        finish(1, 0, S)
+        ours(2, 0, S)
+        theirs(2, 0, S, False)
+        neighbour(3, 0, HALF, False)
+        weight(3, HALF, S)
+        ours(3, 0, HALF)
+        finish(2, 0, S)
+        theirs(3, 0, HALF, False)
+        ours(3, HALF, S)
+        finish(3, 0, HALF)
+        theirs(3, HALF, S, True)
+        finish(3, HALF, S)

@@ -183,6 +183,9 @@ def tile_picked_twkeyjointbtrack_none_p_kernel(
             else:
                 nc.scalar.copy(h_rows[t][:, lo:hi], h_acc[t][:, lo:hi])
 
+        warm = keep.tile([P, 8], F32, name="warm")
+        nc.gpsimd.memset(warm[:, 0:1], 0.0)
+        nc.scalar.activation(warm[:, 4:5], warm[:, 0:1], ACT.Sigmoid)
         nc.scalar.copy(d_rows[0][:, :S], d_acc[0][:])
         difference(0, 0, S)
         nc.scalar.copy(d_rows[1][:, :S], d_acc[1][:])

@@ -14,12 +14,13 @@ ALU = mybir.AluOpType
 
 P = 128
 PACK = 4
-K = 512
 TABLE = 2048
 S = 512
 HALF = S // 2
+GROUP = 16
+QUADRANT = 32
 SPARE = 16
-FLOPS = 3 * 2 * 512 * 512 * 512
+FLOPS = 3 * 2 * S * S * S
 
 
 def tile_picked_twkeyjointbtrack_none_p_kernel(
@@ -28,11 +29,10 @@ def tile_picked_twkeyjointbtrack_none_p_kernel(
     nc = tc.nc
     with ExitStack() as ctx:
         keep = ctx.enter_context(tc.tile_pool(name="keep", bufs=1))
-        ring = ctx.enter_context(tc.tile_pool(name="ring", bufs=3))
         psum = ctx.enter_context(tc.psum_pool(name="psum", bufs=1))
 
         def load_list(name, src):
-            tile = keep.tile([P, S // 16], U16, name=name)
+            tile = keep.tile([P, S // GROUP], U16, name=name)
             nc.sync.dma_start(tile[:], src)
             return tile
 
@@ -46,6 +46,37 @@ def tile_picked_twkeyjointbtrack_none_p_kernel(
             nc.sync.dma_start(tile[:], src.rearrange("(p j) n -> p j n", j=PACK))
             return tile
 
+        def gather(name, dtype, table, lst, tag):
+            tile = keep.tile([P, S], dtype, name=name, tag=tag, align_bytes=64)
+            nc.vector.tensor_copy(tile[:], table[:].indirect(lst[:]))
+            return tile
+
+        def quantize(name, grouped, width):
+            codes = keep.tile([P, width], U32, name=name + "_codes", align_bytes=64)
+            scales = keep.tile([P, width], U8, name=name + "_scales", align_bytes=64)
+            nc.vector.quantize_mx(out=codes[:].bitcast(FP8X4), scales=scales[:], in_=grouped[:])
+            return codes, scales
+
+        def product(dst, stationary, t, moving):
+            cols = slice(t * P, (t + 1) * P)
+            nc.tensor.matmul_mx(
+                out=dst,
+                lhsT=stationary[0][:, cols].bitcast(FP8X4),
+                lhsT_scale=stationary[1][:, cols],
+                rhs=moving[0][:].bitcast(FP8X4),
+                rhs_scale=moving[1][:],
+                start=True,
+                stop=True,
+            )
+
+        def row_tile(name):
+            tile = keep.tile([P, S + SPARE], F32, name=name)
+            nc.gpsimd.memset(tile[:, S:], 0.0)
+            return tile
+
+        def look_up(rows, lst, lo, hi):
+            return rows[:].indirect(lst[:, lo // GROUP : hi // GROUP])
+
         ds_table = keep.tile([P, TABLE], U8, name="ds_table", align_bytes=64)
         xs_table = keep.tile([P, TABLE], U8, name="xs_table", align_bytes=64)
         d_scale = keep.tile([P, S], U8, name="d_scale", align_bytes=64)
@@ -58,122 +89,95 @@ def tile_picked_twkeyjointbtrack_none_p_kernel(
         n1_l = load_list("n1_l", n1)
         ds_rows = d_scales[0].bitcast(I32)
         for e in range(2):
-            nc.sync.dma_start(ds_table[:].bitcast(I32)[e:P:16, :], ds_rows[e:16:2, :])
+            nc.sync.dma_start(ds_table[:].bitcast(I32)[e:P:GROUP, :], ds_rows[e:16:2, :])
         dw_table = load_words("dw_table", d_words)
         xs_rows = x_scales[0].bitcast(I32)
-        for q in range(4):
-            nc.sync.dma_start(xs_table[:].bitcast(I32)[32 * q : 32 * q + 4, :], xs_rows[4 * q : 4 * q + 4, :])
-        n3_l = load_list("n3_l", n3)
-        n4_l = load_list("n4_l", n4)
+        for r in range(4):
+            nc.sync.dma_start(xs_table[:].bitcast(I32)[r:P:QUADRANT, :], xs_rows[r:16:4, :])
         xw_table = load_words("xw_table", x_words)
         offs_l = load_list("offs_l", offs)
+        n3_l = load_list("n3_l", n3)
+        n4_l = load_list("n4_l", n4)
         gain = keep.tile([P, PACK], F32, name="gain")
         nc.gpsimd.dma_start(gain[:], gn.rearrange("(p t) o -> p (t o)", t=PACK))
 
-        def gather(name, dtype, table, lst, tag=None):
-            tile = keep.tile([P, S], dtype, name=name, tag=tag or name, align_bytes=64)
-            nc.vector.tensor_copy(tile[:], table[:].indirect(lst[:]))
-            return tile
-
-        def quantize(name, grouped, width):
-            codes = keep.tile([P, width], U32, name=name + "_codes", align_bytes=64)
-            scales = keep.tile([P, width], U8, name=name + "_scales", align_bytes=64)
-            nc.vector.quantize_mx(out=codes[:].bitcast(FP8X4), scales=scales[:], in_=grouped[:])
-            return codes, scales
-
-        def product(dst, stat, t, moving):
-            cols = slice(t * P, (t + 1) * P)
-            nc.tensor.matmul_mx(
-                out=dst, lhsT=stat[0][:, cols].bitcast(FP8X4), lhsT_scale=stat[1][:, cols],
-                rhs=moving[0][:].bitcast(FP8X4), rhs_scale=moving[1][:], start=True, stop=True,
-            )
-
-        ds_picked = gather("ds_picked", U8, ds_table, k1_l, tag="weight")
+        ds_picked = gather("ds_picked", U8, ds_table, k1_l, "staging")
         nc.vector.tensor_copy(
             d_scale[:].rearrange("p (t m) -> p t m", t=PACK), ds_picked[:].rearrange("p (m t) -> p t m", t=PACK)
         )
         for e in range(2):
-            nc.sync.dma_start(d_scale[:].bitcast(I32)[2 + e : P : 32, :], d_scale[:].bitcast(I32)[16 + e : P : 32, :])
-        w1_raw = load_weight("w1_raw", w1, "weight")
+            nc.sync.dma_start(
+                d_scale[:].bitcast(I32)[2 + e : P : QUADRANT, :], d_scale[:].bitcast(I32)[GROUP + e : P : QUADRANT, :]
+            )
+        w1_raw = load_weight("w1_raw", w1, "staging")
 
-        dw_picked = gather("dw_picked", U32, dw_table, k1_l)
-        xs_two = gather("xs_two", U8, xs_table, two_l)
+        dw_picked = gather("dw_picked", U32, dw_table, k1_l, "dw_picked")
+        xs_two = gather("xs_two", U8, xs_table, two_l, "xs_two")
         d_codes = keep.tile([P, S], U32, name="d_codes", align_bytes=64)
         nc.vector.tensor_copy(
             d_codes[:].rearrange("p (t a b) -> p a t b", t=PACK, b=4),
             dw_picked[:].rearrange("p (a b t) -> p a t b", t=PACK, b=4),
         )
-        xw_two = gather("xw_two", U32, xw_table, two_l)
-        d_acc = []
+        xw_two = gather("xw_two", U32, xw_table, two_l, "xw_two")
+        d_acc = [psum.tile([P, S], F32, name="d_acc%d" % t, tag="d_then_h%d" % t) for t in range(PACK)]
         for t in range(PACK):
-            acc = psum.tile([P, S], F32, name="d_acc%d" % t, tag="left%d" % t)
-            product(acc[:], (d_codes, d_scale), t, (xw_two, xs_two))
-            d_acc.append(acc)
-        xs_offs = gather("xs_offs", U8, xs_table, offs_l)
-        xw_offs = gather("xw_offs", U32, xw_table, offs_l)
+            product(d_acc[t][:], (d_codes, d_scale), t, (xw_two, xs_two))
 
-        y_acc = []
-        w2_q = []
+        xs_offs = gather("xs_offs", U8, xs_table, offs_l, "xs_offs")
+        xw_offs = gather("xw_offs", U32, xw_table, offs_l, "xw_offs")
+        w1_grouped = keep.tile([P, PACK * S], BF16, name="w1_grouped", align_bytes=64)
+        nc.vector.tensor_copy(
+            w1_grouped[:].rearrange("p (t m j) -> p m t j", t=PACK, j=PACK),
+            w1_raw[:].rearrange("p j (m t) -> p m t j", t=PACK),
+        )
+        w1_q = quantize("w1", w1_grouped, S)
+        y_acc = [psum.tile([P, S], F32, name="y_acc%d" % t, tag="y%d" % t) for t in range(PACK)]
+        for t in range(PACK):
+            product(y_acc[t][:], w1_q, t, (xw_offs, xs_offs))
 
-        def first_layer():
-            w1_grouped = keep.tile([P, PACK * S], BF16, name="w1_grouped", align_bytes=64)
-            nc.vector.tensor_copy(
-                w1_grouped[:].rearrange("p (t m j) -> p m t j", t=PACK, j=PACK),
-                w1_raw[:].rearrange("p j (m t) -> p m t j", t=PACK),
+        d_rows = [row_tile("d_row%d" % t) for t in range(PACK)]
+        h_rows = [row_tile("h_row%d" % t) for t in range(PACK)]
+        y_gain = keep.tile([P, PACK, S], F32, name="y_gain")
+        minus = keep.tile([P, PACK, S], F32, name="minus")
+        diff = keep.tile([P, PACK, S], F32, name="diff", tag="staging", align_bytes=64)
+        gate = keep.tile([P, 2, PACK, HALF], F32, name="gate")
+
+        def fetch_d(t):
+            nc.scalar.copy(d_rows[t][:, :S], d_acc[t][:])
+
+        def difference(t, lo, hi):
+            nc.scalar.activation(minus[:, t, lo:hi], look_up(d_rows[t], n2_l, lo, hi), ACT.Copy, scale=-1.0)
+            nc.vector.tensor_tensor(diff[:, t, lo:hi], look_up(d_rows[t], n1_l, lo, hi), minus[:, t, lo:hi], ALU.add)
+
+        def squash(t, lo, hi):
+            nc.scalar.activation(
+                gate[:, lo // HALF : hi // HALF, t, :],
+                diff[:, t, lo:hi].rearrange("p (f c) -> p f c", c=HALF),
+                ACT.Tanh,
+                scale=0.0625,
             )
-            w1_q = quantize("w1", w1_grouped, S)
-            for t in range(PACK):
-                acc = psum.tile([P, S], F32, name="y_acc%d" % t, tag="right%d" % t)
-                product(acc[:], w1_q, t, (xw_offs, xs_offs))
-                y_acc.append(acc)
 
-        def second_weights():
+        def fetch_y(t):
+            nc.scalar.activation(y_gain[:, t, :], y_acc[t][:], ACT.Copy, scale=gain[:, t : t + 1])
+
+        def quantize_w2():
             w2_raw = load_weight("w2_raw", w2, "dw_table")
             w2_grouped = keep.tile([P, PACK * S], BF16, name="w2_grouped", align_bytes=64)
             nc.vector.tensor_copy(
                 w2_grouped[:].rearrange("p (c i j) -> p c j i", i=4, j=PACK),
                 w2_raw[:].rearrange("p j (c i) -> p c j i", i=4),
             )
-            w2_q.extend(quantize("w2", w2_grouped, S))
+            return quantize("w2", w2_grouped, S)
 
-        def window(name):
-            tile = keep.tile([P, S + SPARE], F32, name=name)
-            nc.gpsimd.memset(tile[:, S:], 0.0)
-            return tile
-
-        def entries(lst, lo, hi):
-            return lst[:, lo // 16 : hi // 16]
-
-        first_layer()
-        d_rows = [window("d_row%d" % t) for t in range(PACK)]
-        h_rows = [window("h_row%d" % t) for t in range(PACK)]
-        y_gain = keep.tile([P, PACK, S], F32, name="y_gain")
-        minus = keep.tile([P, PACK, S], F32, name="minus")
-        diff = keep.tile([P, PACK, S], F32, name="diff", tag="weight", align_bytes=64)
-        gate = keep.tile([P, PACK, S], F32, name="gate")
-        h_acc = []
-
-        def difference(t, lo, hi):
-            nc.scalar.activation(minus[:, t, lo:hi], d_rows[t][:].indirect(entries(n2_l, lo, hi)), ACT.Copy, scale=-1.0)
-            nc.vector.tensor_tensor(
-                diff[:, t, lo:hi], d_rows[t][:].indirect(entries(n1_l, lo, hi)), minus[:, t, lo:hi], ALU.add
-            )
-
-        def squash(t, lo, hi):
-            nc.scalar.activation(gate[:, t, lo:hi], diff[:, t, lo:hi], ACT.Tanh, scale=0.0625)
-
-        def gained(t):
-            nc.scalar.activation(y_gain[:, t, :], y_acc[t][:], ACT.Copy, scale=gain[:, t : t + 1])
-
-        def second_layer(lo, hi):
-            z_grouped = keep.tile([P, PACK * (hi - lo)], BF16, name="z_grouped%d" % lo, align_bytes=64)
+        def last_product(lo, hi):
+            z_grouped = keep.tile([P, PACK * HALF], BF16, name="z_grouped%d" % lo, align_bytes=64)
             nc.vector.tensor_tensor(
                 z_grouped[:].rearrange("p (c i t) -> p c t i", i=2, t=PACK),
                 y_gain[:, :, lo:hi].rearrange("p t (c i) -> p c t i", i=2),
-                gate[:, :, lo:hi].rearrange("p t (c i) -> p c t i", i=2),
+                gate[:, lo // HALF, :, :].rearrange("p t (c i) -> p c t i", i=2),
                 ALU.mult,
             )
-            z_q = quantize("z%d" % lo, z_grouped, hi - lo)
+            z_q = quantize("z%d" % lo, z_grouped, HALF)
             for t in range(PACK):
                 product(h_acc[t][:, lo:hi], w2_q, t, z_q)
 
@@ -186,91 +190,90 @@ def tile_picked_twkeyjointbtrack_none_p_kernel(
         warm = keep.tile([P, 8], F32, name="warm")
         nc.gpsimd.memset(warm[:, 0:1], 0.0)
         nc.scalar.activation(warm[:, 4:5], warm[:, 0:1], ACT.Sigmoid)
-        nc.scalar.copy(d_rows[0][:, :S], d_acc[0][:])
+
+        fetch_d(0)
         difference(0, 0, S)
-        nc.scalar.copy(d_rows[1][:, :S], d_acc[1][:])
+        fetch_d(1)
         difference(1, 0, S)
         squash(0, 0, S)
-        nc.scalar.copy(d_rows[2][:, :S], d_acc[2][:])
+        fetch_d(2)
         difference(2, 0, HALF)
-        nc.scalar.copy(d_rows[3][:, :S], d_acc[3][:])
+        fetch_d(3)
         difference(3, 0, HALF)
         squash(1, 0, S)
-        for t in range(PACK):
-            h_acc.append(psum.tile([P, S], F32, name="h_acc%d" % t, tag="left%d" % t))
-        gained(0)
-        gained(1)
-        second_weights()
+        h_acc = [psum.tile([P, S], F32, name="h_acc%d" % t, tag="d_then_h%d" % t) for t in range(PACK)]
+        fetch_y(0)
+        fetch_y(1)
+        w2_q = quantize_w2()
         squash(2, 0, HALF)
-        gained(2)
+        fetch_y(2)
         squash(3, 0, HALF)
-        gained(3)
+        fetch_y(3)
         difference(2, HALF, S)
-        second_layer(0, HALF)
+        last_product(0, HALF)
         difference(3, HALF, S)
         squash(2, HALF, S)
         squash(3, HALF, S)
         for t in range(PACK):
             fetch_h(t, 0, HALF, False)
-        second_layer(HALF, S)
+        last_product(HALF, S)
 
         mix = keep.tile([P, PACK, S], F32, name="mix")
         other = keep.tile([P, PACK, S], F32, name="other")
-        first = keep.tile([P, PACK, S], F32, name="first")
-        part = keep.tile([P, PACK, S], F32, name="part")
+        their_part = keep.tile([P, PACK, S], F32, name="their_part")
+        own_part = keep.tile([P, PACK, S], F32, name="own_part")
         result = keep.tile([P, PACK, S], F32, name="result")
 
-        def weight(t, lo, hi):
-            nc.scalar.activation(mix[:, t, lo:hi], h_rows[t][:].indirect(entries(n3_l, lo, hi)), ACT.Sigmoid)
+        def make_mix(t, lo, hi):
+            nc.scalar.activation(mix[:, t, lo:hi], look_up(h_rows[t], n3_l, lo, hi), ACT.Sigmoid)
 
-        def neighbour(t, lo, hi, on_vector):
-            looked_up = h_rows[t][:].indirect(entries(n4_l, lo, hi))
+        def fetch_other(t, lo, hi, on_vector):
             if on_vector:
-                nc.vector.tensor_copy(other[:, t, lo:hi], looked_up)
+                nc.vector.tensor_copy(other[:, t, lo:hi], look_up(h_rows[t], n4_l, lo, hi))
             else:
-                nc.scalar.activation(other[:, t, lo:hi], looked_up, ACT.Copy)
+                nc.scalar.activation(other[:, t, lo:hi], look_up(h_rows[t], n4_l, lo, hi), ACT.Copy)
 
-        def theirs(t, lo, hi, fused):
-            src = h_rows[t][:].indirect(entries(n4_l, lo, hi)) if fused else other[:, t, lo:hi]
-            nc.vector.tensor_tensor(first[:, t, lo:hi], src, mix[:, t, lo:hi], ALU.mult)
+        def make_theirs(t, lo, hi, fused):
+            src = look_up(h_rows[t], n4_l, lo, hi) if fused else other[:, t, lo:hi]
+            nc.vector.tensor_tensor(their_part[:, t, lo:hi], src, mix[:, t, lo:hi], ALU.mult)
 
-        def ours(t, lo, hi):
+        def make_own(t, lo, hi):
             nc.vector.scalar_tensor_tensor(
-                part[:, t, lo:hi], mix[:, t, lo:hi], 1.0, h_acc[t][:, lo:hi], ALU.subtract, ALU.mult
+                own_part[:, t, lo:hi], mix[:, t, lo:hi], 1.0, h_acc[t][:, lo:hi], ALU.subtract, ALU.mult
             )
 
         def finish(t, lo, hi):
-            nc.vector.tensor_tensor(result[:, t, lo:hi], first[:, t, lo:hi], part[:, t, lo:hi], ALU.subtract)
+            nc.vector.tensor_tensor(result[:, t, lo:hi], their_part[:, t, lo:hi], own_part[:, t, lo:hi], ALU.subtract)
             nc.sync.dma_start(out[t * P : (t + 1) * P, lo:hi], result[:, t, lo:hi])
 
         fetch_h(0, HALF, S, True)
-        weight(0, 0, HALF)
-        neighbour(0, 0, HALF, True)
-        weight(0, HALF, S)
+        make_mix(0, 0, HALF)
+        fetch_other(0, 0, HALF, True)
+        make_mix(0, HALF, S)
         fetch_h(1, HALF, S, False)
-        theirs(0, 0, HALF, False)
-        weight(1, 0, HALF)
-        theirs(0, HALF, S, True)
-        weight(1, HALF, S)
-        ours(0, 0, S)
+        make_theirs(0, 0, HALF, False)
+        make_mix(1, 0, HALF)
+        make_theirs(0, HALF, S, True)
+        make_mix(1, HALF, S)
+        make_own(0, 0, S)
         fetch_h(2, HALF, S, False)
-        theirs(1, 0, S, True)
+        make_theirs(1, 0, S, True)
         finish(0, 0, S)
-        weight(2, 0, HALF)
-        weight(2, HALF, S)
-        ours(1, 0, S)
-        neighbour(2, 0, S, False)
+        make_mix(2, 0, HALF)
+        make_mix(2, HALF, S)
+        make_own(1, 0, S)
+        fetch_other(2, 0, S, False)
         fetch_h(3, HALF, S, False)
-        weight(3, 0, HALF)
+        make_mix(3, 0, HALF)
         finish(1, 0, S)
-        ours(2, 0, S)
-        theirs(2, 0, S, False)
-        neighbour(3, 0, HALF, False)
-        weight(3, HALF, S)
-        ours(3, 0, HALF)
+        make_own(2, 0, S)
+        make_theirs(2, 0, S, False)
+        fetch_other(3, 0, HALF, False)
+        make_mix(3, HALF, S)
+        make_own(3, 0, HALF)
         finish(2, 0, S)
-        theirs(3, 0, HALF, False)
-        ours(3, HALF, S)
+        make_theirs(3, 0, HALF, False)
+        make_own(3, HALF, S)
         finish(3, 0, HALF)
-        theirs(3, HALF, S, True)
+        make_theirs(3, HALF, S, True)
         finish(3, HALF, S)

from contextlib import ExitStack

import concourse.mybir as mybir

F32 = mybir.dt.float32
BF16 = mybir.dt.bfloat16
I32 = mybir.dt.int32
U32 = mybir.dt.uint32
U16 = mybir.dt.uint16
U8 = mybir.dt.uint8
FP8X4 = mybir.dt.float8_e4m3fn_x4
ACT = mybir.ActivationFunctionType
ALU = mybir.AluOpType

P = 128
PACK = 4
TABLE = 2048
S = 512
HALF = S // 2
GROUP = 16
QUADRANT = 32
SPARE = 16
FLOPS = 3 * 2 * S * S * S


def tile_picked_twkeyjointbtrack_none_p_kernel(
    tc, x_words, x_scales, w1, d_words, d_scales, gn, w2, offs, k1, two, n1, n2, n3, n4, out
):
    nc = tc.nc
    with ExitStack() as ctx:
        keep = ctx.enter_context(tc.tile_pool(name="keep", bufs=1))
        psum = ctx.enter_context(tc.psum_pool(name="psum", bufs=1))

        def load_list(name, src):
            tile = keep.tile([P, S // GROUP], U16, name=name)
            nc.sync.dma_start(tile[:], src)
            return tile

        def load_words(name, src):
            tile = keep.tile([P, TABLE], U32, name=name, tag=name, align_bytes=64)
            nc.sync.dma_start(tile[:].bitcast(I32), src[0].rearrange("p c r -> p (c r)").bitcast(I32))
            return tile

        def load_weight(name, src, tag):
            tile = keep.tile([P, PACK, S], F32, name=name, tag=tag, align_bytes=64)
            nc.sync.dma_start(tile[:], src.rearrange("(p j) n -> p j n", j=PACK))
            return tile

        def gather(name, dtype, table, lst, tag):
            tile = keep.tile([P, S], dtype, name=name, tag=tag, align_bytes=64)
            nc.vector.tensor_copy(tile[:], table[:].indirect(lst[:]))
            return tile

        def quantize(name, grouped, width):
            codes = keep.tile([P, width], U32, name=name + "_codes", align_bytes=64)
            scales = keep.tile([P, width], U8, name=name + "_scales", align_bytes=64)
            nc.vector.quantize_mx(out=codes[:].bitcast(FP8X4), scales=scales[:], in_=grouped[:])
            return codes, scales

        def product(dst, stationary, t, moving):
            cols = slice(t * P, (t + 1) * P)
            nc.tensor.matmul_mx(
                out=dst,
                lhsT=stationary[0][:, cols].bitcast(FP8X4),
                lhsT_scale=stationary[1][:, cols],
                rhs=moving[0][:].bitcast(FP8X4),
                rhs_scale=moving[1][:],
                start=True,
                stop=True,
            )

        def row_tile(name):
            tile = keep.tile([P, S + SPARE], F32, name=name)
            nc.gpsimd.memset(tile[:, S:], 0.0)
            return tile

        def look_up(rows, lst, lo, hi):
            return rows[:].indirect(lst[:, lo // GROUP : hi // GROUP])

        ds_table = keep.tile([P, TABLE], U8, name="ds_table", align_bytes=64)
        xs_table = keep.tile([P, TABLE], U8, name="xs_table", align_bytes=64)
        d_scale = keep.tile([P, S], U8, name="d_scale", align_bytes=64)
        nc.vector.memset(ds_table[:].bitcast(I32), 0)
        nc.vector.memset(xs_table[:].bitcast(I32), 0)

        k1_l = load_list("k1_l", k1)
        two_l = load_list("two_l", two)
        n2_l = load_list("n2_l", n2)
        n1_l = load_list("n1_l", n1)
        ds_rows = d_scales[0].bitcast(I32)
        for e in range(2):
            nc.sync.dma_start(ds_table[:].bitcast(I32)[e:P:GROUP, :], ds_rows[e:16:2, :])
        dw_table = load_words("dw_table", d_words)
        xs_rows = x_scales[0].bitcast(I32)
        for r in range(4):
            nc.sync.dma_start(xs_table[:].bitcast(I32)[r:P:QUADRANT, :], xs_rows[r:16:4, :])
        xw_table = load_words("xw_table", x_words)
        offs_l = load_list("offs_l", offs)
        n3_l = load_list("n3_l", n3)
        n4_l = load_list("n4_l", n4)
        gain = keep.tile([P, PACK], F32, name="gain")
        nc.gpsimd.dma_start(gain[:], gn.rearrange("(p t) o -> p (t o)", t=PACK))

        ds_picked = gather("ds_picked", U8, ds_table, k1_l, "staging")
        nc.vector.tensor_copy(
            d_scale[:].rearrange("p (t m) -> p t m", t=PACK), ds_picked[:].rearrange("p (m t) -> p t m", t=PACK)
        )
        for e in range(2):
            nc.sync.dma_start(
                d_scale[:].bitcast(I32)[2 + e : P : QUADRANT, :], d_scale[:].bitcast(I32)[GROUP + e : P : QUADRANT, :]
            )
        w1_raw = load_weight("w1_raw", w1, "staging")

        dw_picked = gather("dw_picked", U32, dw_table, k1_l, "dw_picked")
        xs_two = gather("xs_two", U8, xs_table, two_l, "xs_two")
        d_codes = keep.tile([P, S], U32, name="d_codes", align_bytes=64)
        nc.vector.tensor_copy(
            d_codes[:].rearrange("p (t a b) -> p a t b", t=PACK, b=4),
            dw_picked[:].rearrange("p (a b t) -> p a t b", t=PACK, b=4),
        )
        xw_two = gather("xw_two", U32, xw_table, two_l, "xw_two")
        d_acc = [psum.tile([P, S], F32, name="d_acc%d" % t, tag="d_then_h%d" % t) for t in range(PACK)]
        for t in range(PACK):
            product(d_acc[t][:], (d_codes, d_scale), t, (xw_two, xs_two))

        xs_offs = gather("xs_offs", U8, xs_table, offs_l, "xs_offs")
        xw_offs = gather("xw_offs", U32, xw_table, offs_l, "xw_offs")
        w1_grouped = keep.tile([P, PACK * S], BF16, name="w1_grouped", align_bytes=64)
        nc.vector.tensor_copy(
            w1_grouped[:].rearrange("p (t m j) -> p m t j", t=PACK, j=PACK),
            w1_raw[:].rearrange("p j (m t) -> p m t j", t=PACK),
        )
        w1_q = quantize("w1", w1_grouped, S)
        y_acc = [psum.tile([P, S], F32, name="y_acc%d" % t, tag="y%d" % t) for t in range(PACK)]
        for t in range(PACK):
            product(y_acc[t][:], w1_q, t, (xw_offs, xs_offs))

        d_rows = [row_tile("d_row%d" % t) for t in range(PACK)]
        h_rows = [row_tile("h_row%d" % t) for t in range(PACK)]
        y_gain = keep.tile([P, PACK, S], F32, name="y_gain")
        minus = keep.tile([P, PACK, S], F32, name="minus")
        diff = keep.tile([P, PACK, S], F32, name="diff", tag="staging", align_bytes=64)
        gate = keep.tile([P, 2, PACK, HALF], F32, name="gate")

        def fetch_d(t):
            nc.scalar.copy(d_rows[t][:, :S], d_acc[t][:])

        def difference(t, lo, hi):
            nc.scalar.activation(minus[:, t, lo:hi], look_up(d_rows[t], n2_l, lo, hi), ACT.Copy, scale=-1.0)
            nc.vector.tensor_tensor(diff[:, t, lo:hi], look_up(d_rows[t], n1_l, lo, hi), minus[:, t, lo:hi], ALU.add)

        def squash(t, lo, hi):
            nc.scalar.activation(
                gate[:, lo // HALF : hi // HALF, t, :],
                diff[:, t, lo:hi].rearrange("p (f c) -> p f c", c=HALF),
                ACT.Tanh,
                scale=0.0625,
            )

        def fetch_y(t):
            nc.scalar.activation(y_gain[:, t, :], y_acc[t][:], ACT.Copy, scale=gain[:, t : t + 1])

        def quantize_w2():
            w2_raw = load_weight("w2_raw", w2, "dw_table")
            w2_grouped = keep.tile([P, PACK * S], BF16, name="w2_grouped", align_bytes=64)
            nc.vector.tensor_copy(
                w2_grouped[:].rearrange("p (c i j) -> p c j i", i=4, j=PACK),
                w2_raw[:].rearrange("p j (c i) -> p c j i", i=4),
            )
            return quantize("w2", w2_grouped, S)

        def last_product(lo, hi):
            z_grouped = keep.tile([P, PACK * HALF], BF16, name="z_grouped%d" % lo, align_bytes=64)
            nc.vector.tensor_tensor(
                z_grouped[:].rearrange("p (c i t) -> p c t i", i=2, t=PACK),
                y_gain[:, :, lo:hi].rearrange("p t (c i) -> p c t i", i=2),
                gate[:, lo // HALF, :, :].rearrange("p t (c i) -> p c t i", i=2),
                ALU.mult,
            )
            z_q = quantize("z%d" % lo, z_grouped, HALF)
            for t in range(PACK):
                product(h_acc[t][:, lo:hi], w2_q, t, z_q)

        def fetch_h(t, lo, hi, on_vector):
            if on_vector:
                nc.vector.tensor_copy(h_rows[t][:, lo:hi], h_acc[t][:, lo:hi])
            else:
                nc.scalar.copy(h_rows[t][:, lo:hi], h_acc[t][:, lo:hi])

        warm = keep.tile([P, 8], F32, name="warm")
        nc.gpsimd.memset(warm[:, 0:1], 0.0)
        nc.scalar.activation(warm[:, 4:5], warm[:, 0:1], ACT.Sigmoid)

        fetch_d(0)
        difference(0, 0, S)
        fetch_d(1)
        difference(1, 0, S)
        squash(0, 0, S)
        fetch_d(2)
        difference(2, 0, HALF)
        fetch_d(3)
        difference(3, 0, HALF)
        squash(1, 0, S)
        h_acc = [psum.tile([P, S], F32, name="h_acc%d" % t, tag="d_then_h%d" % t) for t in range(PACK)]
        fetch_y(0)
        fetch_y(1)
        w2_q = quantize_w2()
        squash(2, 0, HALF)
        fetch_y(2)
        squash(3, 0, HALF)
        fetch_y(3)
        difference(2, HALF, S)
        last_product(0, HALF)
        difference(3, HALF, S)
        squash(2, HALF, S)
        squash(3, HALF, S)
        for t in range(PACK):
            fetch_h(t, 0, HALF, False)
        last_product(HALF, S)

        mix = keep.tile([P, PACK, S], F32, name="mix")
        other = keep.tile([P, PACK, S], F32, name="other")
        their_part = keep.tile([P, PACK, S], F32, name="their_part")
        own_part = keep.tile([P, PACK, S], F32, name="own_part")
        result = keep.tile([P, PACK, S], F32, name="result")

        def make_mix(t, lo, hi):
            nc.scalar.activation(mix[:, t, lo:hi], look_up(h_rows[t], n3_l, lo, hi), ACT.Sigmoid)

        def fetch_other(t, lo, hi, on_vector):
            if on_vector:
                nc.vector.tensor_copy(other[:, t, lo:hi], look_up(h_rows[t], n4_l, lo, hi))
            else:
                nc.scalar.activation(other[:, t, lo:hi], look_up(h_rows[t], n4_l, lo, hi), ACT.Copy)

        def make_theirs(t, lo, hi, fused):
            src = look_up(h_rows[t], n4_l, lo, hi) if fused else other[:, t, lo:hi]
            nc.vector.tensor_tensor(their_part[:, t, lo:hi], src, mix[:, t, lo:hi], ALU.mult)

        def make_own(t, lo, hi):
            nc.vector.scalar_tensor_tensor(
                own_part[:, t, lo:hi], mix[:, t, lo:hi], 1.0, h_acc[t][:, lo:hi], ALU.subtract, ALU.mult
            )

        def finish(t, lo, hi):
            nc.vector.tensor_tensor(result[:, t, lo:hi], their_part[:, t, lo:hi], own_part[:, t, lo:hi], ALU.subtract)
            nc.sync.dma_start(out[t * P : (t + 1) * P, lo:hi], result[:, t, lo:hi])

        fetch_h(0, HALF, S, True)
        make_mix(0, 0, HALF)
        fetch_other(0, 0, HALF, True)
        make_mix(0, HALF, S)
        fetch_h(1, HALF, S, False)
        make_theirs(0, 0, HALF, False)
        make_mix(1, 0, HALF)
        make_theirs(0, HALF, S, True)
        make_mix(1, HALF, S)
        make_own(0, 0, S)
        fetch_h(2, HALF, S, False)
        make_theirs(1, 0, S, True)
        finish(0, 0, S)
        make_mix(2, 0, HALF)
        make_mix(2, HALF, S)
        make_own(1, 0, S)
        fetch_other(2, 0, S, False)
        fetch_h(3, HALF, S, False)
        make_mix(3, 0, HALF)
        finish(1, 0, S)
        make_own(2, 0, S)
        make_theirs(2, 0, S, False)
        fetch_other(3, 0, HALF, False)
        make_mix(3, HALF, S)
        make_own(3, 0, HALF)
        finish(2, 0, S)
        make_theirs(3, 0, HALF, False)
        make_own(3, HALF, S)
        finish(3, 0, HALF)
        make_theirs(3, HALF, S, True)
        finish(3, HALF, S)
